import numpy as np
import ml_dtypes


def mxq(x, axis, fmt="e4m3"):
    dtype, down = {"e4m3": (ml_dtypes.float8_e4m3fn, 7), "e5m2": (ml_dtypes.float8_e5m2, 14)}[fmt]
    v = np.moveaxis(np.asarray(x, np.float32).astype(ml_dtypes.bfloat16).astype(np.float64), axis, -1)
    blocks = v.reshape(v.shape[:-1] + (-1, 32))
    amax = np.abs(blocks).max(-1, keepdims=True)
    byte = np.maximum(np.where(amax > 0, np.frexp(amax)[1] - 1 + 127, 0) - down, 1)
    scale = np.exp2(byte - 127.0)
    codes = (blocks / scale).astype(np.float32).astype(dtype).astype(np.float64)
    return np.moveaxis((codes * scale).reshape(v.shape), -1, axis)


WIDE = False


def mx_kscale(k):
    if not WIDE:
        return np.ones(k)
    levels = np.array([10, -10, 5, -5, 0])
    if k % 512:
        return np.exp2(np.random.permutation(np.resize(levels, k // 32))).repeat(32)
    a = np.empty((k // 512, 16))
    for p in range(k // 512):
        a[p, :8] = np.random.permutation(np.resize(levels, 8))
        for g in range(8):
            far = levels[np.abs(levels - a[p, g]) >= 10]
            a[p, g + 8] = far[np.random.randint(len(far))]
    return np.exp2(a.ravel()).repeat(32)


def f64(x):
    return np.asarray(x).astype(np.float64)


def striped(idx):
    return np.tile(np.asarray(idx).reshape(-1, 16).T, (8, 1)).astype(np.uint16)


def unstriped(offs):
    return offs[:16].T.reshape(-1).astype(np.int64)


def striped8(idx):
    return np.asarray(idx).reshape(8, -1, 16).transpose(0, 2, 1).reshape(128, -1).astype(np.uint16)


def unstriped8(offs):
    return offs.reshape(8, 16, -1).transpose(0, 2, 1).reshape(8, -1).astype(np.int64)


def pick8(x, idx, run):
    r = np.arange(len(x))
    return x[r[:, None], idx[r % (8 * run) // run]]


E2M1 = np.array([0.0, 0.5, 1.0, 1.5, 2.0, 3.0, 4.0, 6.0, -0.0, -0.5, -1.0, -1.5, -2.0, -3.0, -4.0, -6.0])


def pack_weight(w, fmt):
    k, n = w.shape
    w = f64(np.asarray(w, np.float32).astype(ml_dtypes.bfloat16)).reshape(k // 32, 32, n)
    amax = np.abs(w).max(1)
    if fmt == "e4m3":
        byte = np.frexp(amax)[1] - 1 + 127 - 7
    else:
        mant, ex = np.frexp(amax / 6.0)
        byte = np.where(mant > 0.5, ex, ex - 1) + 127
    byte = np.clip(np.where(amax > 0, byte, 1), 1, 254)
    scaled = (w * np.exp2(127.0 - byte)[:, None, :]).reshape(k, n).astype(np.float32)
    by_word = np.ascontiguousarray(scaled.reshape(k // 512, 128, 4, n).transpose(0, 1, 3, 2))
    if fmt == "e4m3":
        words = by_word.astype(ml_dtypes.float8_e4m3fn).view(np.uint8)
    else:
        c = by_word.astype(ml_dtypes.float4_e2m1fn).view(np.uint8) & 0xF
        words = (c[..., 0::2] | (c[..., 1::2] << 4)).reshape(k // 512, 128, 2 * n)
    return np.ascontiguousarray(words), np.ascontiguousarray(byte.astype(np.uint8).reshape(k // 512, 16, n))


def unpack_weight(words, scales, fmt):
    g, _, n = scales.shape
    words = np.ascontiguousarray(words).reshape(g, 128, n, -1)
    if fmt == "e4m3":
        vals = words.view(ml_dtypes.float8_e4m3fn).astype(np.float64)
    else:
        nib = np.empty((g, 128, n, 4), np.uint8)
        nib[..., 0::2] = words & 0xF
        nib[..., 1::2] = words >> 4
        vals = E2M1[nib]
    vals = vals * np.repeat(np.exp2(scales.astype(np.float64) - 127.0), 8, axis=1)[..., None]
    return vals.transpose(0, 1, 3, 2).reshape(g * 512, n)


def sgn(shape):
    return np.random.uniform(0.5, 2.0, shape) * np.where(np.random.standard_normal(shape) < 0, -1.0, 1.0)


K, J, R, T, F, G, O, N, U, E = 512, 512, 512, 1024, 1024, 1024, 256, 256, 128, 512


def setup_inputs():
    n = np.random.standard_normal
    idx = np.random.permutation(T)[:J]
    idx2 = np.random.permutation(F)[:R]
    idx3 = np.stack([np.random.permutation(G)[:R] for _ in range(8)])
    idx4 = np.stack([np.random.permutation(J)[:O] for _ in range(8)])
    idx5 = np.random.permutation(T)[:O]
    idx6 = np.stack([np.random.permutation(O)[:U] for _ in range(8)])
    idx7 = np.stack([np.random.permutation(E)[:U] for _ in range(8)])
    fk = mx_kscale(K)
    fr = mx_kscale(R)
    xtp = pack_weight(n((K, T)) * fk[:, None], "e4m3")
    wbp = pack_weight(n((R, N)) * 1 / np.sqrt(R) / fr[:, None], "e4m3")
    wsp = pack_weight(n((K, N)) * 1 / np.sqrt(K) / fk[:, None], "e2m1")
    return {
        "xt_words": xtp[0],
        "xt_scales": xtp[1],
        "ua": (np.random.randint(-7, 8, (K, F)).astype(np.float64)).astype(np.float32),
        "ub": (np.random.randint(-7, 8, (K, G)).astype(np.float64)).astype(np.float32),
        "ha": ((np.random.randint(10, 25, (K, 1)) / 1024.0) / fk[:, None]).astype(np.float32),
        "hb": ((np.random.randint(4, 13, (K, 1)) / 1024.0) / fk[:, None]).astype(np.float32),
        "sa": (np.random.uniform(0.5, 1.6, (R, 1)) * fr[:, None]).astype(np.float32),
        "wb_words": wbp[0],
        "wb_scales": wbp[1],
        "ws_words": wsp[0],
        "ws_scales": wsp[1],
        "so": (sgn((N, 1))).astype(np.float32),
        "offs": striped(idx),
        "offs2": striped(idx2),
        "offs3": striped8(idx3),
        "offs4": striped8(idx4),
        "offs5": striped(idx5),
        "offs6": striped8(idx6),
        "offs7": striped8(idx7),
    }


def reference(xt_words, xt_scales, ua, ub, ha, hb, sa, wb_words, wb_scales, ws_words, ws_scales, so, offs, offs2, offs3, offs4, offs5, offs6, offs7):
    idx = unstriped(offs)
    idx2 = unstriped(offs2)
    idx3 = unstriped8(offs3)
    idx4 = unstriped8(offs4)
    idx5 = unstriped(offs5)
    idx6 = unstriped8(offs6)
    idx7 = unstriped8(offs7)
    xtu = unpack_weight(xt_words, xt_scales, "e4m3")
    wbu = unpack_weight(wb_words, wb_scales, "e4m3")
    wsu = unpack_weight(ws_words, ws_scales, "e2m1")
    wc = f64(ua)[:, idx2] * f64(ha) + pick8(f64(ub), idx3, 64) * f64(hb)
    wcq = mxq(wc, 0, "e4m3")
    xtidxg = xtu[:, idx]
    a = wcq.T @ xtidxg
    g1 = np.maximum(a, 0.0)
    hid = pick8(g1, idx4, 64) * f64(sa)
    hidq = mxq(hid, 0, "e4m3")
    xtidx5g = xtu[:, idx5]
    p = wbu.T @ hidq + wsu.T @ xtidx5g
    m0 = pick8(p, idx6, 16) * f64(so)
    y = np.zeros((N, E))
    y[np.arange(N)[:, None], idx7[np.arange(N) % 128 // 16]] = m0
    return y

@@ -1,0 +1,206 @@
+from contextlib import ExitStack
+
+import concourse.mybir as mybir
+
+F32 = mybir.dt.float32
+BF16 = mybir.dt.bfloat16
+I32 = mybir.dt.int32
+U32 = mybir.dt.uint32
+U16 = mybir.dt.uint16
+U8 = mybir.dt.uint8
+FP8X4 = mybir.dt.float8_e4m3fn_x4
+FP4X4 = mybir.dt.float4_e2m1fn_x4
+ACT = mybir.ActivationFunctionType
+ALU = mybir.AluOpType
+
+K, J, R, T, F, G, O, N, U, E = 512, 512, 512, 1024, 1024, 1024, 256, 256, 128, 512
+P = 128
+PACK = 4
+FLOPS = 2 * K * R * J + 2 * R * N * O + 2 * K * N * O
+
+
+def tile_picked_tokens_basedetail_one_kept_further_posted_kernel(
+    tc, xt_words, xt_scales, ua, ub, ha, hb, sa, wb_words, wb_scales, ws_words, ws_scales, so,
+    offs, offs2, offs3, offs4, offs5, offs6, offs7, out,
+):
+    nc = tc.nc
+    with ExitStack() as ctx:
+        keep = ctx.enter_context(tc.tile_pool(name="keep", bufs=1))
+        psum = ctx.enter_context(tc.psum_pool(name="psum", bufs=1))
+
+        def sb(name, shape, dtype):
+            return keep.tile(shape, dtype, name=name, align_bytes=64)
+
+        def load_list(name, src):
+            t = sb(name, list(src.shape), U16)
+            nc.sync.dma_start(t[:], src)
+            return t
+
+        def load_rows(name, src, t):
+            tile = sb(name, [P, src.shape[1]], F32)
+            nc.sync.dma_start(tile[:], src.rearrange("(p t) c -> p t c", t=PACK)[:, t, :])
+            return tile
+
+        def load_column(name, src, queue):
+            tile = sb(name, [P, PACK], F32)
+            queue.dma_start(tile[:], src.rearrange("(p t) o -> p (t o)", t=PACK))
+            return tile
+
+        def load_scale_rows(tile, src, queue):
+            for q in range(4):
+                queue.dma_start(tile[32 * q : 32 * q + 4, :].bitcast(I32), src[0, 4 * q : 4 * q + 4, :].bitcast(I32))
+
+        xs_win = sb("xs_win", [P, T], U8)
+        nc.vector.memset(xs_win[:].bitcast(I32), 0)
+        ws_s = sb("ws_s", [P, N], U8)
+        wb_s = sb("wb_s", [P, N], U8)
+        nc.vector.memset(ws_s[:].bitcast(I32), 0)
+        nc.vector.memset(wb_s[:].bitcast(I32), 0)
+        page = [sb("page%d" % b, [P, E], F32) for b in range(2)]
+        for b in range(2):
+            nc.vector.memset(page[b][:], 0.0)
+
+        ha_t = load_column("ha_t", ha, nc.scalar)
+        hb_t = load_column("hb_t", hb, nc.scalar)
+
+        ua_t, ub_t = [None] * PACK, [None] * PACK
+        ua_t[0] = load_rows("ua0", ua, 0)
+        l2 = load_list("l2", offs2)
+        ub_t[0] = load_rows("ub0", ub, 0)
+        l3 = load_list("l3", offs3)
+        ua_t[1] = load_rows("ua1", ua, 1)
+        ub_t[1] = load_rows("ub1", ub, 1)
+        load_scale_rows(xs_win, xt_scales, nc.sync)
+        l1 = load_list("l1", offs)
+        ua_t[2] = load_rows("ua2", ua, 2)
+        l5 = load_list("l5", offs5)
+        ub_t[2] = load_rows("ub2", ub, 2)
+        xw_win = sb("xw_win", [P, T], I32)
+        nc.sync.dma_start(xw_win[:], xt_words[0].rearrange("p c t -> p (c t)").bitcast(I32))
+        ua_t[3] = load_rows("ua3", ua, 3)
+        ub_t[3] = load_rows("ub3", ub, 3)
+        l4 = load_list("l4", offs4)
+        sa_t = load_column("sa_t", sa, nc.sync)
+        ws_w = sb("ws_w", [P, 2 * N], U8)
+        nc.sync.dma_start(ws_w[:].bitcast(I32), ws_words[0].bitcast(I32))
+        load_scale_rows(ws_s, ws_scales, nc.sync)
+        wb_w = sb("wb_w", [P, N], I32)
+        nc.sync.dma_start(wb_w[:], wb_words[0].rearrange("p c t -> p (c t)").bitcast(I32))
+        load_scale_rows(wb_s, wb_scales, nc.sync)
+        so_t = sb("so_t", [P, 2], F32)
+        with nc.allow_non_contiguous_dma(reason="one value a partition for each of the two row blocks"):
+            nc.sync.dma_start(so_t[:], so.rearrange("(b p) o -> p (b o)", p=P))
+        l6 = load_list("l6", offs6)
+        l7 = load_list("l7", offs7)
+
+        HALF = R // 2
+        base = [sb("base%d" % t, [P, R], F32) for t in range(PACK)]
+        detail = [sb("detail%d" % t, [P, R], F32) for t in range(PACK)]
+        wc = [sb("wc%d" % h, [P, PACK, HALF], BF16) for h in range(2)]
+        xs = sb("xs", [P, J], U8)
+        xw = sb("xw", [P, J], U32)
+        xs5 = sb("xs5", [P, O], U8)
+        xw5 = sb("xw5", [P, O], U32)
+
+        def add_half(t, h):
+            cols = slice(HALF * h, HALF * (h + 1))
+            nc.vector.tensor_tensor(wc[h][:, t, :], base[t][:, cols], detail[t][:, cols], ALU.add)
+
+        for t in range(PACK - 1):
+            nc.scalar.activation(out=base[t][:], in_=ua_t[t][:].indirect(l2[:]), func=ACT.Copy, scale=ha_t[:, t : t + 1])
+            nc.scalar.activation(out=detail[t][:], in_=ub_t[t][:].indirect(l3[:]), func=ACT.Copy, scale=hb_t[:, t : t + 1])
+            add_half(t, 0)
+            add_half(t, 1)
+            if t == 1:
+                nc.vector.tensor_copy(xs[:], xs_win[:].indirect(l1[:]))
+            if t == 1:
+                nc.vector.tensor_copy(xs5[:], xs_win[:].indirect(l5[:]))
+        nc.vector.tensor_copy(xw[:], xw_win[:].bitcast(U32).indirect(l1[:]))
+        nc.vector.tensor_copy(xw5[:], xw_win[:].bitcast(U32).indirect(l5[:]))
+
+        t = PACK - 1
+        nc.scalar.activation(out=base[t][:], in_=ua_t[t][:].indirect(l2[:]), func=ACT.Copy, scale=ha_t[:, t : t + 1])
+        for h in range(2):
+            nc.scalar.activation(
+                out=detail[t][:, HALF * h : HALF * (h + 1)],
+                in_=ub_t[t][:].indirect(l3[:, 16 * h : 16 * (h + 1)]),
+                func=ACT.Copy, scale=hb_t[:, t : t + 1],
+            )
+
+        grouped = [sb("grouped%d" % u, [P, P, PACK], BF16) for u in range(PACK)]
+        wq = [sb("wq%d" % u, [P, P], U32) for u in range(PACK)]
+        wq_s = [sb("wq_s%d" % u, [P, P], U8) for u in range(PACK)]
+
+        def weave(u, h, copy):
+            copy(grouped[u][:, 64 * h : 64 * (h + 1), :], wc[h][:].rearrange("p t (m u) -> p u m t", u=PACK)[:, u, :, :])
+
+        def quantise(u):
+            nc.vector.quantize_mx(out=wq[u][:].bitcast(FP8X4), scales=wq_s[u][:], in_=grouped[u][:].rearrange("p m t -> p (m t)"))
+
+        acc = [psum.tile([P, J], F32, name="acc%d" % u) for u in range(PACK)]
+        pacc = [[psum.tile([P, P], F32, name="pacc%d%d" % (b, h)) for h in range(2)] for b in range(2)]
+
+        def first_product(u):
+            nc.tensor.matmul_mx(out=acc[u][:], lhsT=wq[u][:].bitcast(FP8X4), lhsT_scale=wq_s[u][:],
+                                rhs=xw[:].bitcast(FP8X4), rhs_scale=xs[:], start=True, stop=True)
+
+        add_half(t, 0)
+        weave(0, 0, nc.vector.tensor_copy)
+        weave(1, 0, nc.vector.tensor_copy)
+        add_half(t, 1)
+        weave(2, 0, nc.scalar.copy)
+        weave(3, 0, nc.scalar.copy)
+        weave(0, 1, nc.vector.tensor_copy)
+        weave(1, 1, nc.vector.tensor_copy)
+        weave(2, 1, nc.scalar.copy)
+        quantise(0)
+        first_product(0)
+        weave(3, 1, nc.vector.tensor_copy)
+        quantise(1)
+        first_product(1)
+        quantise(2)
+        first_product(2)
+        quantise(3)
+        first_product(3)
+        for b in range(2):
+            for h in range(2):
+                nc.tensor.matmul_mx(out=pacc[b][h][:], lhsT=ws_w[:, 2 * P * b : 2 * P * (b + 1)].bitcast(FP4X4),
+                                    lhsT_scale=ws_s[:, P * b : P * (b + 1)],
+                                    rhs=xw5[:, P * h : P * (h + 1)].bitcast(FP8X4), rhs_scale=xs5[:, P * h : P * (h + 1)],
+                                    start=True, stop=False)
+
+
+        g1 = [sb("g1_%d" % u, [P, J], F32) for u in range(PACK)]
+        hid = sb("hid", [P, PACK, O], BF16)
+        for u in range(PACK):
+            if u == 0:
+                nc.scalar.activation(out=g1[u][:], in_=acc[u][:], func=ACT.Relu)
+            else:
+                nc.vector.tensor_scalar_max(g1[u][:], acc[u][:], 0.0)
+            if u < PACK - 1:
+                nc.scalar.activation(out=hid[:, u, :], in_=g1[u][:].indirect(l4[:]), func=ACT.Copy, scale=sa_t[:, u : u + 1])
+            else:
+                for h in range(2):
+                    nc.scalar.activation(out=hid[:, u, P * h : P * (h + 1)], in_=g1[u][:].indirect(l4[:, 8 * h : 8 * (h + 1)]),
+                                         func=ACT.Copy, scale=sa_t[:, u : u + 1])
+
+        hgrouped = [sb("hgrouped%d" % h, [P, P, PACK], BF16) for h in range(2)]
+        hq = [sb("hq%d" % h, [P, P], U32) for h in range(2)]
+        hq_s = [sb("hq_s%d" % h, [P, P], U8) for h in range(2)]
+        pw = [sb("pw%d" % b, [P, O], F32) for b in range(2)]
+        for h in range(2):
+            nc.vector.tensor_copy(hgrouped[h][:], hid[:, :, P * h : P * (h + 1)].rearrange("p u o -> p o u"))
+            nc.vector.quantize_mx(out=hq[h][:].bitcast(FP8X4), scales=hq_s[h][:], in_=hgrouped[h][:].rearrange("p o u -> p (o u)"))
+            for b in range(2):
+                nc.tensor.matmul_mx(out=pacc[b][h][:], lhsT=wb_w[:, P * b : P * (b + 1)].bitcast(FP8X4),
+                                    lhsT_scale=wb_s[:, P * b : P * (b + 1)],
+                                    rhs=hq[h][:].bitcast(FP8X4), rhs_scale=hq_s[h][:], start=False, stop=True)
+        for h in range(2):
+            for b in range(2):
+                copy = nc.vector.tensor_copy if (h, b) == (1, 1) else nc.scalar.copy
+                copy(pw[b][:, P * h : P * (h + 1)], pacc[b][h][:])
+        ends = [sb("ends%d" % b, [P, U], F32) for b in range(2)]
+        for b in range(2):
+            nc.scalar.activation(out=ends[b][:], in_=pw[b][:].indirect(l6[:]), func=ACT.Copy, scale=so_t[:, b : b + 1])
+            nc.vector.tensor_copy(page[b][:].indirect(l7[:]), ends[b][:])
+            nc.sync.dma_start(out[P * b : P * (b + 1), :], page[b][:])

@@ -46,9 +46,9 @@ def tile_picked_tokens_basedetail_one_kept_further_posted_kernel(
             queue.dma_start(tile[:], src.rearrange("(p t) o -> p (t o)", t=PACK))
             return tile
 
-        def load_scale_rows(tile, src, queue):
-            for q in range(4):
-                queue.dma_start(tile[32 * q : 32 * q + 4, :].bitcast(I32), src[0, 4 * q : 4 * q + 4, :].bitcast(I32))
+        def load_scale_rows(tile, src, quadrants=range(4)):
+            for q in quadrants:
+                nc.sync.dma_start(tile[32 * q : 32 * q + 4, :].bitcast(I32), src[0, 4 * q : 4 * q + 4, :].bitcast(I32))
 
         xs_win = sb("xs_win", [P, T], U8)
         nc.vector.memset(xs_win[:].bitcast(I32), 0)
@@ -62,6 +62,9 @@ def tile_picked_tokens_basedetail_one_kept_further_posted_kernel(
 
         ha_t = load_column("ha_t", ha, nc.scalar)
         hb_t = load_column("hb_t", hb, nc.scalar)
+        warm = sb("warm", [P, 8], F32)
+        nc.vector.memset(warm[:, 0:1], 0.0)
+        nc.scalar.activation(out=warm[:, 4:5], in_=warm[:, 0:1], func=ACT.Copy)
 
         ua_t, ub_t = [None] * PACK, [None] * PACK
         ua_t[0] = load_rows("ua0", ua, 0)
@@ -70,23 +73,24 @@ def tile_picked_tokens_basedetail_one_kept_further_posted_kernel(
         l3 = load_list("l3", offs3)
         ua_t[1] = load_rows("ua1", ua, 1)
         ub_t[1] = load_rows("ub1", ub, 1)
-        load_scale_rows(xs_win, xt_scales, nc.sync)
         l1 = load_list("l1", offs)
         ua_t[2] = load_rows("ua2", ua, 2)
-        l5 = load_list("l5", offs5)
-        ub_t[2] = load_rows("ub2", ub, 2)
+        load_scale_rows(xs_win, xt_scales, (0, 1))
         xw_win = sb("xw_win", [P, T], I32)
         nc.sync.dma_start(xw_win[:], xt_words[0].rearrange("p c t -> p (c t)").bitcast(I32))
+        load_scale_rows(xs_win, xt_scales, (2, 3))
+        ub_t[2] = load_rows("ub2", ub, 2)
+        l5 = load_list("l5", offs5)
         ua_t[3] = load_rows("ua3", ua, 3)
         ub_t[3] = load_rows("ub3", ub, 3)
         l4 = load_list("l4", offs4)
         sa_t = load_column("sa_t", sa, nc.sync)
         ws_w = sb("ws_w", [P, 2 * N], U8)
         nc.sync.dma_start(ws_w[:].bitcast(I32), ws_words[0].bitcast(I32))
-        load_scale_rows(ws_s, ws_scales, nc.sync)
+        load_scale_rows(ws_s, ws_scales)
         wb_w = sb("wb_w", [P, N], I32)
         nc.sync.dma_start(wb_w[:], wb_words[0].rearrange("p c t -> p (c t)").bitcast(I32))
-        load_scale_rows(wb_s, wb_scales, nc.sync)
+        load_scale_rows(wb_s, wb_scales)
         so_t = sb("so_t", [P, 2], F32)
         with nc.allow_non_contiguous_dma(reason="one value a partition for each of the two row blocks"):
             nc.sync.dma_start(so_t[:], so.rearrange("(b p) o -> p (b o)", p=P))
@@ -112,10 +116,9 @@ def tile_picked_tokens_basedetail_one_kept_further_posted_kernel(
             add_half(t, 0)
             add_half(t, 1)
             if t == 1:
+                nc.vector.tensor_copy(xw[:], xw_win[:].bitcast(U32).indirect(l1[:]))
                 nc.vector.tensor_copy(xs[:], xs_win[:].indirect(l1[:]))
-            if t == 1:
-                nc.vector.tensor_copy(xs5[:], xs_win[:].indirect(l5[:]))
-        nc.vector.tensor_copy(xw[:], xw_win[:].bitcast(U32).indirect(l1[:]))
+        nc.vector.tensor_copy(xs5[:], xs_win[:].indirect(l5[:]))
         nc.vector.tensor_copy(xw5[:], xw_win[:].bitcast(U32).indirect(l5[:]))
 
         t = PACK - 1
@@ -137,12 +140,17 @@ def tile_picked_tokens_basedetail_one_kept_further_posted_kernel(
         def quantise(u):
             nc.vector.quantize_mx(out=wq[u][:].bitcast(FP8X4), scales=wq_s[u][:], in_=grouped[u][:].rearrange("p m t -> p (m t)"))
 
-        acc = [psum.tile([P, J], F32, name="acc%d" % u) for u in range(PACK)]
-        pacc = [[psum.tile([P, P], F32, name="pacc%d%d" % (b, h)) for h in range(2)] for b in range(2)]
+        SPLIT = range(PACK)
+        acc = {}
+        for u in range(PACK):
+            for c in range(2 if u in SPLIT else 1):
+                acc[u, c] = psum.tile([P, J // 2 if u in SPLIT else J], F32, name="acc%d%d" % (u, c), tag="bank%d%d" % (u, c))
 
-        def first_product(u):
-            nc.tensor.matmul_mx(out=acc[u][:], lhsT=wq[u][:].bitcast(FP8X4), lhsT_scale=wq_s[u][:],
-                                rhs=xw[:].bitcast(FP8X4), rhs_scale=xs[:], start=True, stop=True)
+        def first_product(u, c=0):
+            width = acc[u, c].shape[1]
+            cols = slice(width * c, width * (c + 1))
+            nc.tensor.matmul_mx(out=acc[u, c][:], lhsT=wq[u][:].bitcast(FP8X4), lhsT_scale=wq_s[u][:],
+                                rhs=xw[:, cols].bitcast(FP8X4), rhs_scale=xs[:, cols], start=True, stop=True)
 
         add_half(t, 0)
         weave(0, 0, nc.vector.tensor_copy)
@@ -153,36 +161,44 @@ def tile_picked_tokens_basedetail_one_kept_further_posted_kernel(
         weave(0, 1, nc.vector.tensor_copy)
         weave(1, 1, nc.vector.tensor_copy)
         weave(2, 1, nc.scalar.copy)
+        weave(3, 1, nc.scalar.copy)
         quantise(0)
-        first_product(0)
-        weave(3, 1, nc.vector.tensor_copy)
+        first_product(0, 0)
+        first_product(0, 1)
         quantise(1)
-        first_product(1)
+        first_product(1, 0)
+        first_product(1, 1)
         quantise(2)
-        first_product(2)
+        first_product(2, 0)
+        first_product(2, 1)
         quantise(3)
-        first_product(3)
-        for b in range(2):
-            for h in range(2):
-                nc.tensor.matmul_mx(out=pacc[b][h][:], lhsT=ws_w[:, 2 * P * b : 2 * P * (b + 1)].bitcast(FP4X4),
-                                    lhsT_scale=ws_s[:, P * b : P * (b + 1)],
-                                    rhs=xw5[:, P * h : P * (h + 1)].bitcast(FP8X4), rhs_scale=xs5[:, P * h : P * (h + 1)],
-                                    start=True, stop=False)
-
+        first_product(3, 0)
+        first_product(3, 1)
 
         g1 = [sb("g1_%d" % u, [P, J], F32) for u in range(PACK)]
         hid = sb("hid", [P, PACK, O], BF16)
         for u in range(PACK):
-            if u == 0:
-                nc.scalar.activation(out=g1[u][:], in_=acc[u][:], func=ACT.Relu)
-            else:
-                nc.vector.tensor_scalar_max(g1[u][:], acc[u][:], 0.0)
+            for c in range(2 if u in SPLIT else 1):
+                width = acc[u, c].shape[1]
+                cols = slice(width * c, width * (c + 1))
+                if u == 0:
+                    nc.scalar.activation(out=g1[u][:, cols], in_=acc[u, c][:], func=ACT.Relu)
+                else:
+                    nc.vector.tensor_scalar_max(g1[u][:, cols], acc[u, c][:], 0.0)
             if u < PACK - 1:
                 nc.scalar.activation(out=hid[:, u, :], in_=g1[u][:].indirect(l4[:]), func=ACT.Copy, scale=sa_t[:, u : u + 1])
             else:
                 for h in range(2):
                     nc.scalar.activation(out=hid[:, u, P * h : P * (h + 1)], in_=g1[u][:].indirect(l4[:, 8 * h : 8 * (h + 1)]),
                                          func=ACT.Copy, scale=sa_t[:, u : u + 1])
+
+        pacc = [[psum.tile([P, P], F32, name="pacc%d%d" % (b, h), tag="bank%d%d" % (h, b)) for h in range(2)] for b in range(2)]
+        for h in range(2):
+            for b in range(2):
+                nc.tensor.matmul_mx(out=pacc[b][h][:], lhsT=ws_w[:, 2 * P * b : 2 * P * (b + 1)].bitcast(FP4X4),
+                                    lhsT_scale=ws_s[:, P * b : P * (b + 1)],
+                                    rhs=xw5[:, P * h : P * (h + 1)].bitcast(FP8X4), rhs_scale=xs5[:, P * h : P * (h + 1)],
+                                    start=True, stop=False)
 
         hgrouped = [sb("hgrouped%d" % h, [P, P, PACK], BF16) for h in range(2)]
         hq = [sb("hq%d" % h, [P, P], U32) for h in range(2)]
@@ -197,7 +213,7 @@ def tile_picked_tokens_basedetail_one_kept_further_posted_kernel(
                                     rhs=hq[h][:].bitcast(FP8X4), rhs_scale=hq_s[h][:], start=False, stop=True)
         for h in range(2):
             for b in range(2):
-                copy = nc.vector.tensor_copy if (h, b) == (1, 1) else nc.scalar.copy
+                copy = nc.vector.tensor_copy if b == 1 else nc.scalar.copy
                 copy(pw[b][:, P * h : P * (h + 1)], pacc[b][h][:])
         ends = [sb("ends%d" % b, [P, U], F32) for b in range(2)]
         for b in range(2):

@@ -28,8 +28,8 @@ def tile_picked_tokens_basedetail_one_kept_further_posted_kernel(
         keep = ctx.enter_context(tc.tile_pool(name="keep", bufs=1))
         psum = ctx.enter_context(tc.psum_pool(name="psum", bufs=1))
 
-        def sb(name, shape, dtype):
-            return keep.tile(shape, dtype, name=name, align_bytes=64)
+        def sb(name, shape, dtype, tag=None):
+            return keep.tile(shape, dtype, name=name, tag=tag or name, align_bytes=64)
 
         def load_list(name, src):
             t = sb(name, list(src.shape), U16)
@@ -76,13 +76,13 @@ def tile_picked_tokens_basedetail_one_kept_further_posted_kernel(
         l1 = load_list("l1", offs)
         ua_t[2] = load_rows("ua2", ua, 2)
         load_scale_rows(xs_win, xt_scales, (0, 1))
+        ub_t[2] = load_rows("ub2", ub, 2)
+        load_scale_rows(xs_win, xt_scales, (2, 3))
+        ua_t[3] = load_rows("ua3", ua, 3)
+        l5 = load_list("l5", offs5)
+        ub_t[3] = load_rows("ub3", ub, 3)
         xw_win = sb("xw_win", [P, T], I32)
         nc.sync.dma_start(xw_win[:], xt_words[0].rearrange("p c t -> p (c t)").bitcast(I32))
-        load_scale_rows(xs_win, xt_scales, (2, 3))
-        ub_t[2] = load_rows("ub2", ub, 2)
-        l5 = load_list("l5", offs5)
-        ua_t[3] = load_rows("ua3", ua, 3)
-        ub_t[3] = load_rows("ub3", ub, 3)
         l4 = load_list("l4", offs4)
         sa_t = load_column("sa_t", sa, nc.sync)
         ws_w = sb("ws_w", [P, 2 * N], U8)
@@ -104,7 +104,6 @@ def tile_picked_tokens_basedetail_one_kept_further_posted_kernel(
         xs = sb("xs", [P, J], U8)
         xw = sb("xw", [P, J], U32)
         xs5 = sb("xs5", [P, O], U8)
-        xw5 = sb("xw5", [P, O], U32)
 
         def add_half(t, h):
             cols = slice(HALF * h, HALF * (h + 1))
@@ -116,10 +115,8 @@ def tile_picked_tokens_basedetail_one_kept_further_posted_kernel(
             add_half(t, 0)
             add_half(t, 1)
             if t == 1:
-                nc.vector.tensor_copy(xw[:], xw_win[:].bitcast(U32).indirect(l1[:]))
                 nc.vector.tensor_copy(xs[:], xs_win[:].indirect(l1[:]))
         nc.vector.tensor_copy(xs5[:], xs_win[:].indirect(l5[:]))
-        nc.vector.tensor_copy(xw5[:], xw_win[:].bitcast(U32).indirect(l5[:]))
 
         t = PACK - 1
         nc.scalar.activation(out=base[t][:], in_=ua_t[t][:].indirect(l2[:]), func=ACT.Copy, scale=ha_t[:, t : t + 1])
@@ -130,7 +127,7 @@ def tile_picked_tokens_basedetail_one_kept_further_posted_kernel(
                 func=ACT.Copy, scale=hb_t[:, t : t + 1],
             )
 
-        grouped = [sb("grouped%d" % u, [P, P, PACK], BF16) for u in range(PACK)]
+        grouped = [sb("grouped%d" % u, [P, P, PACK], BF16) for u in range(PACK - 1)]
         wq = [sb("wq%d" % u, [P, P], U32) for u in range(PACK)]
         wq_s = [sb("wq_s%d" % u, [P, P], U8) for u in range(PACK)]
 
@@ -152,22 +149,28 @@ def tile_picked_tokens_basedetail_one_kept_further_posted_kernel(
             nc.tensor.matmul_mx(out=acc[u, c][:], lhsT=wq[u][:].bitcast(FP8X4), lhsT_scale=wq_s[u][:],
                                 rhs=xw[:, cols].bitcast(FP8X4), rhs_scale=xs[:, cols], start=True, stop=True)
 
+        def gather_words(c):
+            nc.vector.tensor_copy(xw[:, 256 * c : 256 * (c + 1)], xw_win[:].bitcast(U32).indirect(l1[:, 16 * c : 16 * (c + 1)]))
+
         add_half(t, 0)
         weave(0, 0, nc.vector.tensor_copy)
-        weave(1, 0, nc.vector.tensor_copy)
         add_half(t, 1)
+        weave(1, 0, nc.scalar.copy)
+        gather_words(0)
+        weave(0, 1, nc.scalar.copy)
+        weave(1, 1, nc.scalar.copy)
         weave(2, 0, nc.scalar.copy)
-        weave(3, 0, nc.scalar.copy)
-        weave(0, 1, nc.vector.tensor_copy)
-        weave(1, 1, nc.vector.tensor_copy)
         weave(2, 1, nc.scalar.copy)
-        weave(3, 1, nc.scalar.copy)
         quantise(0)
         first_product(0, 0)
+        gather_words(1)
         first_product(0, 1)
         quantise(1)
         first_product(1, 0)
         first_product(1, 1)
+        grouped.append(sb("grouped3", [P, P, PACK], BF16, tag="grouped0"))
+        weave(3, 0, nc.vector.tensor_copy)
+        weave(3, 1, nc.vector.tensor_copy)
         quantise(2)
         first_product(2, 0)
         first_product(2, 1)
@@ -192,6 +195,8 @@ def tile_picked_tokens_basedetail_one_kept_further_posted_kernel(
                     nc.scalar.activation(out=hid[:, u, P * h : P * (h + 1)], in_=g1[u][:].indirect(l4[:, 8 * h : 8 * (h + 1)]),
                                          func=ACT.Copy, scale=sa_t[:, u : u + 1])
 
+        xw5 = sb("xw5", [P, O], U32, tag="wq3")
+        nc.vector.tensor_copy(xw5[:], xw_win[:].bitcast(U32).indirect(l5[:]))
         pacc = [[psum.tile([P, P], F32, name="pacc%d%d" % (b, h), tag="bank%d%d" % (h, b)) for h in range(2)] for b in range(2)]
         for h in range(2):
             for b in range(2):

from contextlib import ExitStack

import concourse.mybir as mybir

F32 = mybir.dt.float32
BF16 = mybir.dt.bfloat16
I32 = mybir.dt.int32
U32 = mybir.dt.uint32
U16 = mybir.dt.uint16
U8 = mybir.dt.uint8
FP8X4 = mybir.dt.float8_e4m3fn_x4
FP4X4 = mybir.dt.float4_e2m1fn_x4
ACT = mybir.ActivationFunctionType
ALU = mybir.AluOpType

K, J, R, T, F, G, O, N, U, E = 512, 512, 512, 1024, 1024, 1024, 256, 256, 128, 512
P = 128
PACK = 4
FLOPS = 2 * K * R * J + 2 * R * N * O + 2 * K * N * O


def tile_picked_tokens_basedetail_one_kept_further_posted_kernel(
    tc, xt_words, xt_scales, ua, ub, ha, hb, sa, wb_words, wb_scales, ws_words, ws_scales, so,
    offs, offs2, offs3, offs4, offs5, offs6, offs7, out,
):
    nc = tc.nc
    with ExitStack() as ctx:
        keep = ctx.enter_context(tc.tile_pool(name="keep", bufs=1))
        psum = ctx.enter_context(tc.psum_pool(name="psum", bufs=1))

        def sb(name, shape, dtype, tag=None):
            return keep.tile(shape, dtype, name=name, tag=tag or name, align_bytes=64)

        def load_list(name, src):
            t = sb(name, list(src.shape), U16)
            nc.sync.dma_start(t[:], src)
            return t

        def load_rows(name, src, t):
            tile = sb(name, [P, src.shape[1]], F32)
            nc.sync.dma_start(tile[:], src.rearrange("(p t) c -> p t c", t=PACK)[:, t, :])
            return tile

        def load_column(name, src, queue):
            tile = sb(name, [P, PACK], F32)
            queue.dma_start(tile[:], src.rearrange("(p t) o -> p (t o)", t=PACK))
            return tile

        def load_scale_rows(tile, src, quadrants=range(4)):
            for q in quadrants:
                nc.sync.dma_start(tile[32 * q : 32 * q + 4, :].bitcast(I32), src[0, 4 * q : 4 * q + 4, :].bitcast(I32))

        xs_win = sb("xs_win", [P, T], U8)
        nc.vector.memset(xs_win[:].bitcast(I32), 0)
        ws_s = sb("ws_s", [P, N], U8)
        wb_s = sb("wb_s", [P, N], U8)
        nc.vector.memset(ws_s[:].bitcast(I32), 0)
        nc.vector.memset(wb_s[:].bitcast(I32), 0)
        page = [sb("page%d" % b, [P, E], F32) for b in range(2)]
        for b in range(2):
            nc.vector.memset(page[b][:], 0.0)

        ha_t = load_column("ha_t", ha, nc.scalar)
        hb_t = load_column("hb_t", hb, nc.scalar)
        warm = sb("warm", [P, 8], F32)
        nc.vector.memset(warm[:, 0:1], 0.0)
        nc.scalar.activation(out=warm[:, 4:5], in_=warm[:, 0:1], func=ACT.Copy)

        ua_t, ub_t = [None] * PACK, [None] * PACK
        ua_t[0] = load_rows("ua0", ua, 0)
        l2 = load_list("l2", offs2)
        ub_t[0] = load_rows("ub0", ub, 0)
        l3 = load_list("l3", offs3)
        ua_t[1] = load_rows("ua1", ua, 1)
        ub_t[1] = load_rows("ub1", ub, 1)
        l1 = load_list("l1", offs)
        ua_t[2] = load_rows("ua2", ua, 2)
        load_scale_rows(xs_win, xt_scales, (0, 1))
        ub_t[2] = load_rows("ub2", ub, 2)
        load_scale_rows(xs_win, xt_scales, (2, 3))
        ua_t[3] = load_rows("ua3", ua, 3)
        l5 = load_list("l5", offs5)
        ub_t[3] = load_rows("ub3", ub, 3)
        xw_win = sb("xw_win", [P, T], I32)
        nc.sync.dma_start(xw_win[:], xt_words[0].rearrange("p c t -> p (c t)").bitcast(I32))
        l4 = load_list("l4", offs4)
        sa_t = load_column("sa_t", sa, nc.sync)
        ws_w = sb("ws_w", [P, 2 * N], U8)
        nc.sync.dma_start(ws_w[:].bitcast(I32), ws_words[0].bitcast(I32))
        load_scale_rows(ws_s, ws_scales)
        wb_w = sb("wb_w", [P, N], I32)
        nc.sync.dma_start(wb_w[:], wb_words[0].rearrange("p c t -> p (c t)").bitcast(I32))
        load_scale_rows(wb_s, wb_scales)
        so_t = sb("so_t", [P, 2], F32)
        with nc.allow_non_contiguous_dma(reason="one value a partition for each of the two row blocks"):
            nc.sync.dma_start(so_t[:], so.rearrange("(b p) o -> p (b o)", p=P))
        l6 = load_list("l6", offs6)
        l7 = load_list("l7", offs7)

        HALF = R // 2
        base = [sb("base%d" % t, [P, R], F32) for t in range(PACK)]
        detail = [sb("detail%d" % t, [P, R], F32) for t in range(PACK)]
        wc = [sb("wc%d" % h, [P, PACK, HALF], BF16) for h in range(2)]
        xs = sb("xs", [P, J], U8)
        xw = sb("xw", [P, J], U32)
        xs5 = sb("xs5", [P, O], U8)

        def add_half(t, h):
            cols = slice(HALF * h, HALF * (h + 1))
            nc.vector.tensor_tensor(wc[h][:, t, :], base[t][:, cols], detail[t][:, cols], ALU.add)

        for t in range(PACK - 1):
            nc.scalar.activation(out=base[t][:], in_=ua_t[t][:].indirect(l2[:]), func=ACT.Copy, scale=ha_t[:, t : t + 1])
            nc.scalar.activation(out=detail[t][:], in_=ub_t[t][:].indirect(l3[:]), func=ACT.Copy, scale=hb_t[:, t : t + 1])
            add_half(t, 0)
            add_half(t, 1)
            if t == 1:
                nc.vector.tensor_copy(xs[:], xs_win[:].indirect(l1[:]))
        nc.vector.tensor_copy(xs5[:], xs_win[:].indirect(l5[:]))

        t = PACK - 1
        nc.scalar.activation(out=base[t][:], in_=ua_t[t][:].indirect(l2[:]), func=ACT.Copy, scale=ha_t[:, t : t + 1])
        for h in range(2):
            nc.scalar.activation(
                out=detail[t][:, HALF * h : HALF * (h + 1)],
                in_=ub_t[t][:].indirect(l3[:, 16 * h : 16 * (h + 1)]),
                func=ACT.Copy, scale=hb_t[:, t : t + 1],
            )

        grouped = [sb("grouped%d" % u, [P, P, PACK], BF16) for u in range(PACK - 1)]
        wq = [sb("wq%d" % u, [P, P], U32) for u in range(PACK)]
        wq_s = [sb("wq_s%d" % u, [P, P], U8) for u in range(PACK)]

        def weave(u, h, copy):
            copy(grouped[u][:, 64 * h : 64 * (h + 1), :], wc[h][:].rearrange("p t (m u) -> p u m t", u=PACK)[:, u, :, :])

        def quantise(u):
            nc.vector.quantize_mx(out=wq[u][:].bitcast(FP8X4), scales=wq_s[u][:], in_=grouped[u][:].rearrange("p m t -> p (m t)"))

        SPLIT = range(PACK)
        acc = {}
        for u in range(PACK):
            for c in range(2 if u in SPLIT else 1):
                acc[u, c] = psum.tile([P, J // 2 if u in SPLIT else J], F32, name="acc%d%d" % (u, c), tag="bank%d%d" % (u, c))

        def first_product(u, c=0):
            width = acc[u, c].shape[1]
            cols = slice(width * c, width * (c + 1))
            nc.tensor.matmul_mx(out=acc[u, c][:], lhsT=wq[u][:].bitcast(FP8X4), lhsT_scale=wq_s[u][:],
                                rhs=xw[:, cols].bitcast(FP8X4), rhs_scale=xs[:, cols], start=True, stop=True)

        def gather_words(c):
            nc.vector.tensor_copy(xw[:, 256 * c : 256 * (c + 1)], xw_win[:].bitcast(U32).indirect(l1[:, 16 * c : 16 * (c + 1)]))

        add_half(t, 0)
        weave(0, 0, nc.vector.tensor_copy)
        add_half(t, 1)
        weave(1, 0, nc.scalar.copy)
        gather_words(0)
        weave(0, 1, nc.scalar.copy)
        weave(1, 1, nc.scalar.copy)
        weave(2, 0, nc.scalar.copy)
        weave(2, 1, nc.scalar.copy)
        quantise(0)
        first_product(0, 0)
        gather_words(1)
        first_product(0, 1)
        quantise(1)
        first_product(1, 0)
        first_product(1, 1)
        grouped.append(sb("grouped3", [P, P, PACK], BF16, tag="grouped0"))
        weave(3, 0, nc.vector.tensor_copy)
        weave(3, 1, nc.vector.tensor_copy)
        quantise(2)
        first_product(2, 0)
        first_product(2, 1)
        quantise(3)
        first_product(3, 0)
        first_product(3, 1)

        g1 = [sb("g1_%d" % u, [P, J], F32) for u in range(PACK)]
        hid = sb("hid", [P, PACK, O], BF16)
        for u in range(PACK):
            for c in range(2 if u in SPLIT else 1):
                width = acc[u, c].shape[1]
                cols = slice(width * c, width * (c + 1))
                if u == 0:
                    nc.scalar.activation(out=g1[u][:, cols], in_=acc[u, c][:], func=ACT.Relu)
                else:
                    nc.vector.tensor_scalar_max(g1[u][:, cols], acc[u, c][:], 0.0)
            if u < PACK - 1:
                nc.scalar.activation(out=hid[:, u, :], in_=g1[u][:].indirect(l4[:]), func=ACT.Copy, scale=sa_t[:, u : u + 1])
            else:
                for h in range(2):
                    nc.scalar.activation(out=hid[:, u, P * h : P * (h + 1)], in_=g1[u][:].indirect(l4[:, 8 * h : 8 * (h + 1)]),
                                         func=ACT.Copy, scale=sa_t[:, u : u + 1])

        xw5 = sb("xw5", [P, O], U32, tag="wq3")
        nc.vector.tensor_copy(xw5[:], xw_win[:].bitcast(U32).indirect(l5[:]))
        pacc = [[psum.tile([P, P], F32, name="pacc%d%d" % (b, h), tag="bank%d%d" % (h, b)) for h in range(2)] for b in range(2)]
        for h in range(2):
            for b in range(2):
                nc.tensor.matmul_mx(out=pacc[b][h][:], lhsT=ws_w[:, 2 * P * b : 2 * P * (b + 1)].bitcast(FP4X4),
                                    lhsT_scale=ws_s[:, P * b : P * (b + 1)],
                                    rhs=xw5[:, P * h : P * (h + 1)].bitcast(FP8X4), rhs_scale=xs5[:, P * h : P * (h + 1)],
                                    start=True, stop=False)

        hgrouped = [sb("hgrouped%d" % h, [P, P, PACK], BF16) for h in range(2)]
        hq = [sb("hq%d" % h, [P, P], U32) for h in range(2)]
        hq_s = [sb("hq_s%d" % h, [P, P], U8) for h in range(2)]
        pw = [sb("pw%d" % b, [P, O], F32) for b in range(2)]
        for h in range(2):
            nc.vector.tensor_copy(hgrouped[h][:], hid[:, :, P * h : P * (h + 1)].rearrange("p u o -> p o u"))
            nc.vector.quantize_mx(out=hq[h][:].bitcast(FP8X4), scales=hq_s[h][:], in_=hgrouped[h][:].rearrange("p o u -> p (o u)"))
            for b in range(2):
                nc.tensor.matmul_mx(out=pacc[b][h][:], lhsT=wb_w[:, P * b : P * (b + 1)].bitcast(FP8X4),
                                    lhsT_scale=wb_s[:, P * b : P * (b + 1)],
                                    rhs=hq[h][:].bitcast(FP8X4), rhs_scale=hq_s[h][:], start=False, stop=True)
        for h in range(2):
            for b in range(2):
                copy = nc.vector.tensor_copy if b == 1 else nc.scalar.copy
                copy(pw[b][:, P * h : P * (h + 1)], pacc[b][h][:])
        ends = [sb("ends%d" % b, [P, U], F32) for b in range(2)]
        for b in range(2):
            nc.scalar.activation(out=ends[b][:], in_=pw[b][:].indirect(l6[:]), func=ACT.Copy, scale=so_t[:, b : b + 1])
            nc.vector.tensor_copy(page[b][:].indirect(l7[:]), ends[b][:])
            nc.sync.dma_start(out[P * b : P * (b + 1), :], page[b][:])
